import numpy as np
import ml_dtypes


def mxq(x, axis, fmt="e4m3"):
    dtype, down = {"e4m3": (ml_dtypes.float8_e4m3fn, 7), "e5m2": (ml_dtypes.float8_e5m2, 14)}[fmt]
    v = np.moveaxis(np.asarray(x, np.float32).astype(ml_dtypes.bfloat16).astype(np.float64), axis, -1)
    blocks = v.reshape(v.shape[:-1] + (-1, 32))
    amax = np.abs(blocks).max(-1, keepdims=True)
    byte = np.maximum(np.where(amax > 0, np.frexp(amax)[1] - 1 + 127, 0) - down, 1)
    scale = np.exp2(byte - 127.0)
    codes = (blocks / scale).astype(np.float32).astype(dtype).astype(np.float64)
    return np.moveaxis((codes * scale).reshape(v.shape), -1, axis)


WIDE = False


def mx_kscale(k):
    if not WIDE:
        return np.ones(k)
    levels = np.array([10, -10, 5, -5, 0])
    if k % 512:
        return np.exp2(np.random.permutation(np.resize(levels, k // 32))).repeat(32)
    a = np.empty((k // 512, 16))
    for p in range(k // 512):
        a[p, :8] = np.random.permutation(np.resize(levels, 8))
        for g in range(8):
            far = levels[np.abs(levels - a[p, g]) >= 10]
            a[p, g + 8] = far[np.random.randint(len(far))]
    return np.exp2(a.ravel()).repeat(32)


def f64(x):
    return np.asarray(x).astype(np.float64)


def striped(idx):
    return np.tile(np.asarray(idx).reshape(-1, 16).T, (8, 1)).astype(np.uint16)


def unstriped(offs):
    return offs[:16].T.reshape(-1).astype(np.int64)


E2M1 = np.array([0.0, 0.5, 1.0, 1.5, 2.0, 3.0, 4.0, 6.0, -0.0, -0.5, -1.0, -1.5, -2.0, -3.0, -4.0, -6.0])


def pack_weight(w, fmt):
    k, n = w.shape
    w = f64(np.asarray(w, np.float32).astype(ml_dtypes.bfloat16)).reshape(k // 32, 32, n)
    amax = np.abs(w).max(1)
    if fmt == "e4m3":
        byte = np.frexp(amax)[1] - 1 + 127 - 7
    else:
        mant, ex = np.frexp(amax / 6.0)
        byte = np.where(mant > 0.5, ex, ex - 1) + 127
    byte = np.clip(np.where(amax > 0, byte, 1), 1, 254)
    scaled = (w * np.exp2(127.0 - byte)[:, None, :]).reshape(k, n).astype(np.float32)
    by_word = np.ascontiguousarray(scaled.reshape(k // 512, 128, 4, n).transpose(0, 1, 3, 2))
    if fmt == "e4m3":
        words = by_word.astype(ml_dtypes.float8_e4m3fn).view(np.uint8)
    else:
        c = by_word.astype(ml_dtypes.float4_e2m1fn).view(np.uint8) & 0xF
        words = (c[..., 0::2] | (c[..., 1::2] << 4)).reshape(k // 512, 128, 2 * n)
    return np.ascontiguousarray(words), np.ascontiguousarray(byte.astype(np.uint8).reshape(k // 512, 16, n))


def unpack_weight(words, scales, fmt):
    g, _, n = scales.shape
    words = np.ascontiguousarray(words).reshape(g, 128, n, -1)
    if fmt == "e4m3":
        vals = words.view(ml_dtypes.float8_e4m3fn).astype(np.float64)
    else:
        nib = np.empty((g, 128, n, 4), np.uint8)
        nib[..., 0::2] = words & 0xF
        nib[..., 1::2] = words >> 4
        vals = E2M1[nib]
    vals = vals * np.repeat(np.exp2(scales.astype(np.float64) - 127.0), 8, axis=1)[..., None]
    return vals.transpose(0, 1, 3, 2).reshape(g * 512, n)


def softplus(v):
    return np.log(1.0 + np.exp(v))


def sigmoid(v):
    return 1.0 / (1.0 + np.exp(-v))


D, E, T, I, Q, G = 512, 512, 2048, 512, 128, 64


def setup_inputs():
    n = np.random.standard_normal
    idx = np.random.permutation(T)[:I]
    fd = mx_kscale(D)
    fi = mx_kscale(I)
    ti = np.ones(T)
    ti[idx] = fi
    keysp = pack_weight(n((D, T)) / fd[:, None], "e4m3")
    return {
        "query": (n((D, Q)) * 0.8 / np.sqrt(D) * fd[:, None]).astype(np.float32),
        "query2": (n((D, Q)) * 1.0 / np.sqrt(D) * fd[:, None]).astype(np.float32),
        "keys_words": keysp[0],
        "keys_scales": keysp[1],
        "reserve": (np.random.uniform(2.0, 10.0, (Q, 1))).astype(np.float32),
        "dquery2": (n((D, Q)) * 0.6 / np.sqrt(D) * fd[:, None]).astype(np.float32),
        "os": (np.random.uniform(4.0, 16.0, (1, I)) * fi).astype(np.float32),
        "vals": (n((E, T)) / ti).astype(np.float32),
        "offs": striped(idx),
    }


def reference(query, query2, keys_words, keys_scales, reserve, dquery2, os, vals, offs):
    idx = unstriped(offs)
    keysu = unpack_weight(keys_words, keys_scales, "e4m3")
    queryq = mxq(f64(query), 0, "e4m3")
    keysidxg = keysu[:, idx]
    a = queryq.T @ keysidxg
    query2q = mxq(f64(query2), 0, "e4m3")
    b = query2q.T @ keysidxg
    dquery2q = mxq(f64(dquery2), 0, "e4m3")
    tb = dquery2q.T @ keysidxg
    m1 = b.reshape(Q, G, I // G).mean(axis=2)
    q0 = softplus(m1 * 3.0)
    z = np.sum(q0, axis=1, keepdims=True) + f64(reserve)
    pa = np.exp(a)
    s = pa.reshape(Q, G, I // G).sum(axis=2)
    tm1 = tb.reshape(Q, G, I // G).mean(axis=2)
    tq0 = tm1 * 3.0 * sigmoid(m1 * 3.0)
    tz = np.sum(tq0, axis=1, keepdims=True)
    tr = (tq0 / s - tz * q0 / s / z) / z
    trr = np.repeat(tr, I // G, axis=1)
    tw = trr * pa
    wo1 = tw * f64(os)
    wt1 = wo1.T
    vt1 = f64(vals)[:, idx].T
    wt1q = mxq(wt1, 0, "e4m3")
    vt1q = mxq(vt1, 0, "e4m3")
    o = wt1q.T @ vt1q
    return o

@@ -1,0 +1,242 @@
+from contextlib import ExitStack
+
+import concourse.mybir as mybir
+from concourse.masks import make_identity
+
+D, E, T, I, Q, G = 512, 512, 2048, 512, 128, 64
+FLOPS = 2 * Q * I * D * 3 + 2 * Q * I * E
+
+F32 = mybir.dt.float32
+BF16 = mybir.dt.bfloat16
+I32 = mybir.dt.int32
+U32 = mybir.dt.uint32
+U16 = mybir.dt.uint16
+U8 = mybir.dt.uint8
+FP8X4 = mybir.dt.float8_e4m3fn_x4
+ACT = mybir.ActivationFunctionType
+ALU = mybir.AluOpType
+AX = mybir.AxisListType
+
+P = 128
+PACK = 4
+PAGE = I // G
+HALVES = PAGE // PACK
+BLOCKS = E // P
+POOL_BYTES = 4 * T
+
+
+def tile_attend_ttpagequotas_kernel(tc, query, query2, keys_words, keys_scales, reserve, dquery2, slot_factor, vals, offs, out):
+    nc = tc.nc
+    with ExitStack() as ctx:
+        sb = ctx.enter_context(tc.tile_pool(name="sb", bufs=1))
+        vp = ctx.enter_context(tc.tile_pool(name="vp", bufs=1))
+        ps = ctx.enter_context(tc.psum_pool(name="ps", bufs=1))
+
+        offsets = sb.tile([P, I // 16], U16, name="offsets")
+        nc.sync.dma_start(offsets[:], offs)
+
+        key_bytes = sb.tile([P, T], U8, name="key_bytes", tag="key_bytes", align_bytes=64)
+        nc.gpsimd.memset(key_bytes[:].bitcast(I32), 0)
+
+        def load_rows(src, name):
+            raw = sb.tile([P, PACK, Q], F32, name=name + "_raw", align_bytes=64)
+            nc.sync.dma_start(raw[:], src.rearrange("(p j) q -> p j q", j=PACK))
+            return raw
+
+        q_raw = load_rows(query, "q")
+        scale_rows = keys_scales[0].bitcast(I32).rearrange("(c r) n -> r c n", r=PACK)
+        for r in range(PACK):
+            nc.sync.dma_start(key_bytes[r:P:32, :].bitcast(I32), scale_rows[r])
+        key_words = sb.tile([P, T], U32, name="key_words", align_bytes=64)
+        nc.sync.dma_start(key_words[:].bitcast(I32), keys_words[0].rearrange("p n t -> p (n t)").bitcast(I32))
+        q2_raw = load_rows(query2, "q2")
+        dq2_raw = load_rows(dquery2, "dq2")
+        os_col = sb.tile([P, PACK], F32, name="os_col")
+        nc.sync.dma_start(os_col[:], slot_factor.rearrange("o (p t) -> p (o t)", t=PACK))
+        reserve_col = sb.tile([P, 1], F32, name="reserve_col")
+        nc.sync.dma_start(reserve_col[:], reserve)
+        val_pool = []
+        for j in range(BLOCKS):
+            v = vp.tile([P, T], F32, name=f"val_pool{j}", align_bytes=64, offset=j * POOL_BYTES)
+            nc.sync.dma_start(v[:], vals[j * P : (j + 1) * P, :])
+            val_pool.append(v)
+
+        ident = sb.tile([P, P], F32, name="ident", align_bytes=64)
+        make_identity(nc, ident[:])
+
+        def after_gather(j, at, shape, dtype, name):
+            return vp.tile(shape, dtype, name=name, align_bytes=64, offset=j * POOL_BYTES + at)
+
+        def quantize(grouped, name, behind=None, at=0, tag=None):
+            if behind is None:
+                codes = sb.tile([P, P], U32, name=name + "_codes", tag=tag or name + "_codes", align_bytes=64)
+            else:
+                codes = after_gather(behind, at, [P, P], U32, name + "_codes")
+            scales = sb.tile([P, P], U8, name=name + "_scales", align_bytes=64)
+            nc.vector.quantize_mx(out=codes[:].bitcast(FP8X4), scales=scales[:], in_=grouped[:].rearrange("p c t -> p (c t)"))
+            return codes, scales
+
+        def group_rows(raw, name):
+            grouped = sb.tile([P, Q, PACK], BF16, name=name + "_grouped", align_bytes=64)
+            nc.scalar.copy(grouped[:], raw[:].rearrange("p j q -> p q j"))
+            return grouped
+
+        listed_bytes = sb.tile([P, I], U8, name="listed_bytes", align_bytes=64)
+        nc.vector.tensor_copy(listed_bytes[:], key_bytes[:].indirect(offsets[:]))
+        k_scales = sb.tile([P, I], U8, name="k_scales", align_bytes=64)
+        nc.vector.tensor_copy(
+            k_scales[:].rearrange("p (t s) -> p s t", t=PACK), listed_bytes[:].rearrange("p (s t) -> p s t", t=PACK)
+        )
+        q_mx = quantize(group_rows(q_raw, "q"), "q", tag="key_bytes")
+        k_codes = sb.tile([P, I], U32, name="k_codes", align_bytes=64)
+        nc.vector.tensor_copy(k_codes[:].rearrange("p (t s) -> p s t", t=PACK), key_words[:].indirect(offsets[:]))
+        q2_mx = quantize(group_rows(q2_raw, "q2"), "q2")
+        dq2_mx = quantize(group_rows(dq2_raw, "dq2"), "dq2")
+
+        def product(dst, stationary, codes, scales, start=True, stop=True):
+            nc.tensor.matmul_mx(
+                out=dst,
+                lhsT=stationary[0][:].bitcast(FP8X4),
+                lhsT_scale=stationary[1][:],
+                rhs=codes.bitcast(FP8X4),
+                rhs_scale=scales,
+                start=start,
+                stop=stop,
+            )
+
+        a_bank = ps.tile([P, I], F32, name="a_bank", tag="bank_a")
+        product(a_bank[:], q_mx, k_codes[:], k_scales[:])
+        sum_banks = []
+        for name, mx in (("b", q2_mx), ("tb", dq2_mx)):
+            bank = ps.tile([P, P], F32, name=name + "_bank", tag="bank_" + name)
+            for t in range(PACK):
+                cols = slice(t * P, (t + 1) * P)
+                product(bank[:], mx, k_codes[:, cols], k_scales[:, cols], start=(t == 0), stop=(t == PACK - 1))
+            sum_banks.append(bank)
+
+        def page_sum(bank, total):
+            nc.vector.tensor_reduce(total[:], bank[:].rearrange("p (g h) -> p g h", h=HALVES), AX.X, ALU.add)
+            return total
+
+        def by_page(ap):
+            return ap.rearrange("p (t g h) -> p g t h", t=PACK, h=HALVES)
+
+        def by_place(ap):
+            return ap.rearrange("p (t g h) -> p t g h", t=PACK, h=HALVES)
+
+        neg_max = sb.tile([P, G], F32, name="neg_max")
+        nc.vector.tensor_reduce(neg_max[:], by_page(a_bank[:]), AX.XY, ALU.max, negate=True)
+        b_sum = page_sum(sum_banks[0], sb.tile([P, G], F32, name="b_sum"))
+        a_shift = sb.tile([P, I], F32, name="a_shift", tag="shift")
+        nc.vector.tensor_tensor(
+            by_place(a_shift[:]),
+            by_place(a_bank[:]),
+            neg_max[:].unsqueeze(1).unsqueeze(3).to_broadcast([P, PACK, G, HALVES]),
+            ALU.add,
+        )
+
+        mag = sb.tile([P, G], F32, name="mag")
+        nc.scalar.activation(mag[:], b_sum[:], ACT.Abs, scale=3.0 / PAGE)
+        pos = sb.tile([P, G], F32, name="pos")
+        pos_sum = sb.tile([P, 1], F32, name="pos_sum")
+        nc.scalar.activation(pos[:], b_sum[:], ACT.Relu, scale=3.0 / PAGE, accum_out=pos_sum[:])
+        z_part = sb.tile([P, 1], F32, name="z_part")
+        nc.scalar.activation(z_part[:], pos_sum[:], ACT.Identity, bias=reserve_col[:])
+        small = sb.tile([P, G], F32, name="small")
+        nc.scalar.activation(small[:], mag[:], ACT.Exp, scale=-1.0)
+        th = sb.tile([P, G], F32, name="th")
+        nc.scalar.activation(th[:], mag[:], ACT.Tanh, scale=0.5)
+        pa = sb.tile([P, I], F32, name="pa", align_bytes=64)
+        nc.scalar.activation(pa[:], a_shift[:], ACT.Exp)
+        log_part = sb.tile([P, G], F32, name="log_part", tag="shift")
+        log_sum = sb.tile([P, 1], F32, name="log_sum")
+        nc.scalar.activation(log_part[:], small[:], ACT.Ln, bias=1.0, accum_out=log_sum[:])
+        z = sb.tile([P, 1], F32, name="z")
+        nc.scalar.activation(z[:], log_sum[:], ACT.Identity, bias=z_part[:])
+
+        def value_block(j):
+            listed = sb.tile([P, I], BF16, name=f"listed{j}", tag=f"listed{j}", align_bytes=64)
+            nc.vector.tensor_copy(listed[:], val_pool[j][:].indirect(offsets[:]))
+            words = listed[:].bitcast(F32)
+            turned = ps.tile([P, 2, P], F32, name=f"turned{j}", tag=f"bank_v{j}")
+            for u in range(2):
+                nc.tensor.transpose(turned[:, u, :], words[:, u : I // 2 : 2], ident[:])
+            grouped = sb.tile([P, P, PACK], BF16, name=f"v_grouped{j}", align_bytes=64)
+            nc.scalar.copy(
+                grouped[:].rearrange("p c t -> p (c t)").bitcast(F32).rearrange("p (c u) -> p c u", u=2),
+                turned[:].rearrange("p u c -> p c u"),
+            )
+            return grouped
+
+        pat_bank = ps.tile([P, PACK, Q], F32, name="pat_bank", tag="bank_pat")
+        for t in range(PACK):
+            nc.tensor.transpose(pat_bank[:, t, :], pa[:, t * P : (t + 1) * P], ident[:])
+        pa_os = sb.tile([P, PACK, Q], F32, name="pa_os", align_bytes=64)
+        for t in range(PACK):
+            nc.scalar.activation(pa_os[:, t, :], pat_bank[:, t, :], ACT.Copy, scale=os_col[:, t : t + 1])
+
+        v_grouped = [value_block(0)]
+
+        half_s = sb.tile([P, I // 2], F32, name="half_s")
+        nc.gpsimd.tensor_tensor(half_s[:], pa[:, 0 : I // 2], pa[:, I // 2 : I], ALU.add)
+        quarter_s = sb.tile([P, G, HALVES], F32, name="quarter_s")
+        nc.gpsimd.tensor_tensor(quarter_s[:].rearrange("p g h -> p (g h)"), half_s[:, 0:P], half_s[:, P : 2 * P], ALU.add)
+        page_s = sb.tile([P, G], F32, name="page_s")
+        nc.gpsimd.tensor_tensor(page_s[:], quarter_s[:, :, 0], quarter_s[:, :, 1], ALU.add)
+        tb_sum = page_sum(sum_banks[1], after_gather(0, 0, [P, G], F32, "tb_sum"))
+        num = after_gather(0, 1024, [P, G], F32, "num")
+        nc.vector.scalar_tensor_tensor(num[:], b_sum[:], 0.0, small[:], ALU.is_ge, ALU.max)
+
+        v_grouped.append(value_block(1))
+
+        sig2 = after_gather(1, 1024, [P, G], F32, "sig2")
+        nc.vector.scalar_tensor_tensor(sig2[:], th[:], 1.0, num[:], ALU.add, ALU.mult)
+        inv_s = after_gather(1, 3072, [P, G], F32, "inv_s")
+        nc.vector.reciprocal(inv_s[:], page_s[:])
+        neg_tq = sb.tile([P, G], F32, name="neg_tq")
+        neg_tz = sb.tile([P, 1], F32, name="neg_tz")
+        nc.vector.scalar_tensor_tensor(neg_tq[:], tb_sum[:], -1.5 / PAGE, sig2[:], ALU.mult, ALU.mult, accum_out=neg_tz[:])
+        q0 = after_gather(1, 2048, [P, G], F32, "q0")
+        nc.vector.tensor_tensor(q0[:], log_part[:], pos[:], ALU.add)
+        inv_z = after_gather(1, 4096, [P, 1], F32, "inv_z")
+        nc.vector.reciprocal(inv_z[:], z[:])
+        q0tz = sb.tile([P, G], F32, name="q0tz", tag="listed2", align_bytes=64)
+        nc.vector.tensor_scalar(q0tz[:], q0[:], neg_tz[:], None, ALU.mult)
+        v_mx = [quantize(v_grouped[0], "v0", behind=1)]
+        top = sb.tile([P, G], F32, name="top", tag="listed3", align_bytes=64)
+        nc.vector.scalar_tensor_tensor(top[:], q0tz[:], inv_z[:], neg_tq[:], ALU.mult, ALU.subtract)
+        v_grouped.append(value_block(2))
+        tr2 = after_gather(2, 0, [P, G, HALVES], F32, "tr2")
+        nc.vector.scalar_tensor_tensor(
+            tr2[:],
+            top[:].unsqueeze(2).to_broadcast([P, G, HALVES]),
+            inv_z[:],
+            inv_s[:].unsqueeze(2).to_broadcast([P, G, HALVES]),
+            ALU.mult,
+            ALU.mult,
+        )
+        tr_bank = ps.tile([P, Q], F32, name="tr_bank", tag="bank_b")
+        nc.tensor.transpose(tr_bank[:], tr2[:].rearrange("p g h -> p (g h)"), ident[:])
+        v_grouped.append(value_block(3))
+        w_grouped = after_gather(3, 1024, [P, Q, PACK], BF16, "w_grouped")
+        nc.vector.tensor_tensor(
+            w_grouped[:], tr_bank[:].unsqueeze(2).to_broadcast([P, Q, PACK]), pa_os[:].rearrange("p t q -> p q t"), ALU.mult
+        )
+        v_mx.append(quantize(v_grouped[1], "v1", behind=3))
+        w_mx = quantize(w_grouped, "w")
+        v_mx.append(quantize(v_grouped[2], "v2", behind=3, at=2048))
+
+        early = (BLOCKS - 1) * P
+        o_bank = ps.tile([P, early], F32, name="o_bank", tag="bank_a")
+        for j in range(BLOCKS - 1):
+            product(o_bank[:, j * P : (j + 1) * P], w_mx, v_mx[j][0][:], v_mx[j][1][:])
+        o_early = sb.tile([P, early], F32, name="o_early")
+        nc.scalar.copy(o_early[:], o_bank[:])
+        nc.sync.dma_start(out[:, 0:early], o_early[:])
+
+        last_mx = quantize(v_grouped[BLOCKS - 1], "v3")
+        o_bank_last = ps.tile([P, P], F32, name="o_bank_last", tag="bank_tb")
+        product(o_bank_last[:], w_mx, last_mx[0][:], last_mx[1][:])
+        o_last = sb.tile([P, P], F32, name="o_last")
+        nc.vector.tensor_copy(o_last[:], o_bank_last[:])
+        nc.sync.dma_start(out[:, early:E], o_last[:])

@@ -124,10 +124,10 @@ def tile_attend_ttpagequotas_kernel(tc, query, query2, keys_words, keys_scales, 
         def by_place(ap):
             return ap.rearrange("p (t g h) -> p t g h", t=PACK, h=HALVES)
 
-        neg_max = sb.tile([P, G], F32, name="neg_max")
+        neg_max = sb.tile([P, G], F32, name="neg_max", tag="shift")
         nc.vector.tensor_reduce(neg_max[:], by_page(a_bank[:]), AX.XY, ALU.max, negate=True)
         b_sum = page_sum(sum_banks[0], sb.tile([P, G], F32, name="b_sum"))
-        a_shift = sb.tile([P, I], F32, name="a_shift", tag="shift")
+        a_shift = sb.tile([P, I], F32, name="a_shift")
         nc.vector.tensor_tensor(
             by_place(a_shift[:]),
             by_place(a_bank[:]),
@@ -135,22 +135,26 @@ def tile_attend_ttpagequotas_kernel(tc, query, query2, keys_words, keys_scales, 
             ALU.add,
         )
 
-        mag = sb.tile([P, G], F32, name="mag")
-        nc.scalar.activation(mag[:], b_sum[:], ACT.Abs, scale=3.0 / PAGE)
+        parts = sb.tile([P, 2, G], F32, name="parts")
+        mag = parts[:, 0, :]
+        nc.scalar.activation(mag, b_sum[:], ACT.Abs, scale=3.0 / PAGE)
+        nc.scalar.activation(parts[:, 1, :], b_sum[:], ACT.Relu, scale=-3.0 / PAGE)
         pos = sb.tile([P, G], F32, name="pos")
         pos_sum = sb.tile([P, 1], F32, name="pos_sum")
         nc.scalar.activation(pos[:], b_sum[:], ACT.Relu, scale=3.0 / PAGE, accum_out=pos_sum[:])
         z_part = sb.tile([P, 1], F32, name="z_part")
         nc.scalar.activation(z_part[:], pos_sum[:], ACT.Identity, bias=reserve_col[:])
-        small = sb.tile([P, G], F32, name="small")
-        nc.scalar.activation(small[:], mag[:], ACT.Exp, scale=-1.0)
         th = sb.tile([P, G], F32, name="th")
-        nc.scalar.activation(th[:], mag[:], ACT.Tanh, scale=0.5)
+        nc.scalar.activation(th[:], mag, ACT.Tanh, scale=0.5)
+        exps = sb.tile([P, 2, G], F32, name="exps")
+        nc.scalar.activation(exps[:], parts[:], ACT.Exp, scale=-1.0)
+        small = exps[:, 0, :]
+        num = exps[:, 1, :]
         pa = sb.tile([P, I], F32, name="pa", align_bytes=64)
         nc.scalar.activation(pa[:], a_shift[:], ACT.Exp)
         log_part = sb.tile([P, G], F32, name="log_part", tag="shift")
         log_sum = sb.tile([P, 1], F32, name="log_sum")
-        nc.scalar.activation(log_part[:], small[:], ACT.Ln, bias=1.0, accum_out=log_sum[:])
+        nc.scalar.activation(log_part[:], small, ACT.Ln, bias=1.0, accum_out=log_sum[:])
         z = sb.tile([P, 1], F32, name="z")
         nc.scalar.activation(z[:], log_sum[:], ACT.Identity, bias=z_part[:])
 
@@ -168,14 +172,14 @@ def tile_attend_ttpagequotas_kernel(tc, query, query2, keys_words, keys_scales, 
             )
             return grouped
 
+        v_grouped = [value_block(0)]
+
         pat_bank = ps.tile([P, PACK, Q], F32, name="pat_bank", tag="bank_pat")
         for t in range(PACK):
             nc.tensor.transpose(pat_bank[:, t, :], pa[:, t * P : (t + 1) * P], ident[:])
-        pa_os = sb.tile([P, PACK, Q], F32, name="pa_os", align_bytes=64)
+        pa_os = sb.tile([P, PACK, Q], F32, name="pa_os", tag="listed0", align_bytes=64)
         for t in range(PACK):
             nc.scalar.activation(pa_os[:, t, :], pat_bank[:, t, :], ACT.Copy, scale=os_col[:, t : t + 1])
-
-        v_grouped = [value_block(0)]
 
         half_s = sb.tile([P, I // 2], F32, name="half_s")
         nc.gpsimd.tensor_tensor(half_s[:], pa[:, 0 : I // 2], pa[:, I // 2 : I], ALU.add)
@@ -183,38 +187,37 @@ def tile_attend_ttpagequotas_kernel(tc, query, query2, keys_words, keys_scales, 
         nc.gpsimd.tensor_tensor(quarter_s[:].rearrange("p g h -> p (g h)"), half_s[:, 0:P], half_s[:, P : 2 * P], ALU.add)
         page_s = sb.tile([P, G], F32, name="page_s")
         nc.gpsimd.tensor_tensor(page_s[:], quarter_s[:, :, 0], quarter_s[:, :, 1], ALU.add)
-        tb_sum = page_sum(sum_banks[1], after_gather(0, 0, [P, G], F32, "tb_sum"))
-        num = after_gather(0, 1024, [P, G], F32, "num")
-        nc.vector.scalar_tensor_tensor(num[:], b_sum[:], 0.0, small[:], ALU.is_ge, ALU.max)
+        tb_sum = page_sum(sum_banks[1], sb.tile([P, G], F32, name="tb_sum"))
 
         v_grouped.append(value_block(1))
 
         sig2 = after_gather(1, 1024, [P, G], F32, "sig2")
-        nc.vector.scalar_tensor_tensor(sig2[:], th[:], 1.0, num[:], ALU.add, ALU.mult)
+        nc.vector.scalar_tensor_tensor(sig2[:], th[:], 1.0, num, ALU.add, ALU.mult)
         inv_s = after_gather(1, 3072, [P, G], F32, "inv_s")
         nc.vector.reciprocal(inv_s[:], page_s[:])
         neg_tq = sb.tile([P, G], F32, name="neg_tq")
         neg_tz = sb.tile([P, 1], F32, name="neg_tz")
         nc.vector.scalar_tensor_tensor(neg_tq[:], tb_sum[:], -1.5 / PAGE, sig2[:], ALU.mult, ALU.mult, accum_out=neg_tz[:])
-        q0 = after_gather(1, 2048, [P, G], F32, "q0")
-        nc.vector.tensor_tensor(q0[:], log_part[:], pos[:], ALU.add)
         inv_z = after_gather(1, 4096, [P, 1], F32, "inv_z")
         nc.vector.reciprocal(inv_z[:], z[:])
-        q0tz = sb.tile([P, G], F32, name="q0tz", tag="listed2", align_bytes=64)
-        nc.vector.tensor_scalar(q0tz[:], q0[:], neg_tz[:], None, ALU.mult)
         v_mx = [quantize(v_grouped[0], "v0", behind=1)]
-        top = sb.tile([P, G], F32, name="top", tag="listed3", align_bytes=64)
-        nc.vector.scalar_tensor_tensor(top[:], q0tz[:], inv_z[:], neg_tq[:], ALU.mult, ALU.subtract)
-        v_grouped.append(value_block(2))
-        tr2 = after_gather(2, 0, [P, G, HALVES], F32, "tr2")
-        nc.vector.scalar_tensor_tensor(
+
+        q0 = sb.tile([P, G], F32, name="q0")
+        nc.gpsimd.tensor_tensor(q0[:], log_part[:], pos[:], ALU.add)
+        q0tz = sb.tile([P, G], F32, name="q0tz")
+        nc.gpsimd.tensor_scalar(q0tz[:], q0[:], neg_tz[:], inv_z[:], ALU.mult, ALU.mult)
+        inv_sz = sb.tile([P, G], F32, name="inv_sz")
+        nc.gpsimd.tensor_scalar(inv_sz[:], inv_s[:], inv_z[:], 1.0, ALU.mult, ALU.mult)
+        top = sb.tile([P, G], F32, name="top")
+        nc.gpsimd.tensor_tensor(top[:], q0tz[:], neg_tq[:], ALU.subtract)
+        tr2 = sb.tile([P, G, HALVES], F32, name="tr2", align_bytes=64)
+        nc.gpsimd.tensor_tensor(
             tr2[:],
             top[:].unsqueeze(2).to_broadcast([P, G, HALVES]),
-            inv_z[:],
-            inv_s[:].unsqueeze(2).to_broadcast([P, G, HALVES]),
-            ALU.mult,
+            inv_sz[:].unsqueeze(2).to_broadcast([P, G, HALVES]),
             ALU.mult,
         )
+        v_grouped.append(value_block(2))
         tr_bank = ps.tile([P, Q], F32, name="tr_bank", tag="bank_b")
         nc.tensor.transpose(tr_bank[:], tr2[:].rearrange("p g h -> p (g h)"), ident[:])
         v_grouped.append(value_block(3))
@@ -225,18 +228,16 @@ def tile_attend_ttpagequotas_kernel(tc, query, query2, keys_words, keys_scales, 
         v_mx.append(quantize(v_grouped[1], "v1", behind=3))
         w_mx = quantize(w_grouped, "w")
         v_mx.append(quantize(v_grouped[2], "v2", behind=3, at=2048))
+        v_mx.append(quantize(v_grouped[3], "v3"))
 
-        early = (BLOCKS - 1) * P
-        o_bank = ps.tile([P, early], F32, name="o_bank", tag="bank_a")
-        for j in range(BLOCKS - 1):
-            product(o_bank[:, j * P : (j + 1) * P], w_mx, v_mx[j][0][:], v_mx[j][1][:])
-        o_early = sb.tile([P, early], F32, name="o_early")
-        nc.scalar.copy(o_early[:], o_bank[:])
-        nc.sync.dma_start(out[:, 0:early], o_early[:])
-
-        last_mx = quantize(v_grouped[BLOCKS - 1], "v3")
-        o_bank_last = ps.tile([P, P], F32, name="o_bank_last", tag="bank_tb")
-        product(o_bank_last[:], w_mx, last_mx[0][:], last_mx[1][:])
-        o_last = sb.tile([P, P], F32, name="o_last")
-        nc.vector.tensor_copy(o_last[:], o_bank_last[:])
-        nc.sync.dma_start(out[:, early:E], o_last[:])
+        for first, count, tag, copy in (
+            (0, 2, "bank_a", nc.scalar.copy),
+            (2, 1, "bank_pat", nc.vector.tensor_copy),
+            (3, 1, "bank_tb", nc.vector.tensor_copy),
+        ):
+            o_bank = ps.tile([P, count * P], F32, name=f"o_bank{first}", tag=tag)
+            for j in range(count):
+                product(o_bank[:, j * P : (j + 1) * P], w_mx, v_mx[first + j][0][:], v_mx[first + j][1][:])
+            o_rows = sb.tile([P, count * P], F32, name=f"o_rows{first}")
+            copy(o_rows[:], o_bank[:])
+            nc.sync.dma_start(out[:, first * P : (first + count) * P], o_rows[:])

from contextlib import ExitStack

import concourse.mybir as mybir
from concourse.masks import make_identity

D, E, T, I, Q, G = 512, 512, 2048, 512, 128, 64
FLOPS = 2 * Q * I * D * 3 + 2 * Q * I * E

F32 = mybir.dt.float32
BF16 = mybir.dt.bfloat16
I32 = mybir.dt.int32
U32 = mybir.dt.uint32
U16 = mybir.dt.uint16
U8 = mybir.dt.uint8
FP8X4 = mybir.dt.float8_e4m3fn_x4
ACT = mybir.ActivationFunctionType
ALU = mybir.AluOpType
AX = mybir.AxisListType

P = 128
PACK = 4
PAGE = I // G
HALVES = PAGE // PACK
BLOCKS = E // P
POOL_BYTES = 4 * T


def tile_attend_ttpagequotas_kernel(tc, query, query2, keys_words, keys_scales, reserve, dquery2, slot_factor, vals, offs, out):
    nc = tc.nc
    with ExitStack() as ctx:
        sb = ctx.enter_context(tc.tile_pool(name="sb", bufs=1))
        vp = ctx.enter_context(tc.tile_pool(name="vp", bufs=1))
        ps = ctx.enter_context(tc.psum_pool(name="ps", bufs=1))

        offsets = sb.tile([P, I // 16], U16, name="offsets")
        nc.sync.dma_start(offsets[:], offs)

        key_bytes = sb.tile([P, T], U8, name="key_bytes", tag="key_bytes", align_bytes=64)
        nc.gpsimd.memset(key_bytes[:].bitcast(I32), 0)

        def load_rows(src, name):
            raw = sb.tile([P, PACK, Q], F32, name=name + "_raw", align_bytes=64)
            nc.sync.dma_start(raw[:], src.rearrange("(p j) q -> p j q", j=PACK))
            return raw

        q_raw = load_rows(query, "q")
        scale_rows = keys_scales[0].bitcast(I32).rearrange("(c r) n -> r c n", r=PACK)
        for r in range(PACK):
            nc.sync.dma_start(key_bytes[r:P:32, :].bitcast(I32), scale_rows[r])
        key_words = sb.tile([P, T], U32, name="key_words", align_bytes=64)
        nc.sync.dma_start(key_words[:].bitcast(I32), keys_words[0].rearrange("p n t -> p (n t)").bitcast(I32))
        q2_raw = load_rows(query2, "q2")
        dq2_raw = load_rows(dquery2, "dq2")
        os_col = sb.tile([P, PACK], F32, name="os_col")
        nc.sync.dma_start(os_col[:], slot_factor.rearrange("o (p t) -> p (o t)", t=PACK))
        reserve_col = sb.tile([P, 1], F32, name="reserve_col")
        nc.sync.dma_start(reserve_col[:], reserve)
        val_pool = []
        for j in range(BLOCKS):
            v = vp.tile([P, T], F32, name=f"val_pool{j}", align_bytes=64, offset=j * POOL_BYTES)
            nc.sync.dma_start(v[:], vals[j * P : (j + 1) * P, :])
            val_pool.append(v)

        ident = sb.tile([P, P], F32, name="ident", align_bytes=64)
        make_identity(nc, ident[:])

        def after_gather(j, at, shape, dtype, name):
            return vp.tile(shape, dtype, name=name, align_bytes=64, offset=j * POOL_BYTES + at)

        def quantize(grouped, name, behind=None, at=0, tag=None):
            if behind is None:
                codes = sb.tile([P, P], U32, name=name + "_codes", tag=tag or name + "_codes", align_bytes=64)
            else:
                codes = after_gather(behind, at, [P, P], U32, name + "_codes")
            scales = sb.tile([P, P], U8, name=name + "_scales", align_bytes=64)
            nc.vector.quantize_mx(out=codes[:].bitcast(FP8X4), scales=scales[:], in_=grouped[:].rearrange("p c t -> p (c t)"))
            return codes, scales

        def group_rows(raw, name):
            grouped = sb.tile([P, Q, PACK], BF16, name=name + "_grouped", align_bytes=64)
            nc.scalar.copy(grouped[:], raw[:].rearrange("p j q -> p q j"))
            return grouped

        listed_bytes = sb.tile([P, I], U8, name="listed_bytes", align_bytes=64)
        nc.vector.tensor_copy(listed_bytes[:], key_bytes[:].indirect(offsets[:]))
        k_scales = sb.tile([P, I], U8, name="k_scales", align_bytes=64)
        nc.vector.tensor_copy(
            k_scales[:].rearrange("p (t s) -> p s t", t=PACK), listed_bytes[:].rearrange("p (s t) -> p s t", t=PACK)
        )
        q_mx = quantize(group_rows(q_raw, "q"), "q", tag="key_bytes")
        k_codes = sb.tile([P, I], U32, name="k_codes", align_bytes=64)
        nc.vector.tensor_copy(k_codes[:].rearrange("p (t s) -> p s t", t=PACK), key_words[:].indirect(offsets[:]))
        q2_mx = quantize(group_rows(q2_raw, "q2"), "q2")
        dq2_mx = quantize(group_rows(dq2_raw, "dq2"), "dq2")

        def product(dst, stationary, codes, scales, start=True, stop=True):
            nc.tensor.matmul_mx(
                out=dst,
                lhsT=stationary[0][:].bitcast(FP8X4),
                lhsT_scale=stationary[1][:],
                rhs=codes.bitcast(FP8X4),
                rhs_scale=scales,
                start=start,
                stop=stop,
            )

        a_bank = ps.tile([P, I], F32, name="a_bank", tag="bank_a")
        product(a_bank[:], q_mx, k_codes[:], k_scales[:])
        sum_banks = []
        for name, mx in (("b", q2_mx), ("tb", dq2_mx)):
            bank = ps.tile([P, P], F32, name=name + "_bank", tag="bank_" + name)
            for t in range(PACK):
                cols = slice(t * P, (t + 1) * P)
                product(bank[:], mx, k_codes[:, cols], k_scales[:, cols], start=(t == 0), stop=(t == PACK - 1))
            sum_banks.append(bank)

        def page_sum(bank, total):
            nc.vector.tensor_reduce(total[:], bank[:].rearrange("p (g h) -> p g h", h=HALVES), AX.X, ALU.add)
            return total

        def by_page(ap):
            return ap.rearrange("p (t g h) -> p g t h", t=PACK, h=HALVES)

        def by_place(ap):
            return ap.rearrange("p (t g h) -> p t g h", t=PACK, h=HALVES)

        neg_max = sb.tile([P, G], F32, name="neg_max", tag="shift")
        nc.vector.tensor_reduce(neg_max[:], by_page(a_bank[:]), AX.XY, ALU.max, negate=True)
        b_sum = page_sum(sum_banks[0], sb.tile([P, G], F32, name="b_sum"))
        a_shift = sb.tile([P, I], F32, name="a_shift")
        nc.vector.tensor_tensor(
            by_place(a_shift[:]),
            by_place(a_bank[:]),
            neg_max[:].unsqueeze(1).unsqueeze(3).to_broadcast([P, PACK, G, HALVES]),
            ALU.add,
        )

        parts = sb.tile([P, 2, G], F32, name="parts")
        mag = parts[:, 0, :]
        nc.scalar.activation(mag, b_sum[:], ACT.Abs, scale=3.0 / PAGE)
        nc.scalar.activation(parts[:, 1, :], b_sum[:], ACT.Relu, scale=-3.0 / PAGE)
        pos = sb.tile([P, G], F32, name="pos")
        pos_sum = sb.tile([P, 1], F32, name="pos_sum")
        nc.scalar.activation(pos[:], b_sum[:], ACT.Relu, scale=3.0 / PAGE, accum_out=pos_sum[:])
        z_part = sb.tile([P, 1], F32, name="z_part")
        nc.scalar.activation(z_part[:], pos_sum[:], ACT.Identity, bias=reserve_col[:])
        th = sb.tile([P, G], F32, name="th")
        nc.scalar.activation(th[:], mag, ACT.Tanh, scale=0.5)
        exps = sb.tile([P, 2, G], F32, name="exps")
        nc.scalar.activation(exps[:], parts[:], ACT.Exp, scale=-1.0)
        small = exps[:, 0, :]
        num = exps[:, 1, :]
        pa = sb.tile([P, I], F32, name="pa", align_bytes=64)
        nc.scalar.activation(pa[:], a_shift[:], ACT.Exp)
        log_part = sb.tile([P, G], F32, name="log_part", tag="shift")
        log_sum = sb.tile([P, 1], F32, name="log_sum")
        nc.scalar.activation(log_part[:], small, ACT.Ln, bias=1.0, accum_out=log_sum[:])
        z = sb.tile([P, 1], F32, name="z")
        nc.scalar.activation(z[:], log_sum[:], ACT.Identity, bias=z_part[:])

        def value_block(j):
            listed = sb.tile([P, I], BF16, name=f"listed{j}", tag=f"listed{j}", align_bytes=64)
            nc.vector.tensor_copy(listed[:], val_pool[j][:].indirect(offsets[:]))
            words = listed[:].bitcast(F32)
            turned = ps.tile([P, 2, P], F32, name=f"turned{j}", tag=f"bank_v{j}")
            for u in range(2):
                nc.tensor.transpose(turned[:, u, :], words[:, u : I // 2 : 2], ident[:])
            grouped = sb.tile([P, P, PACK], BF16, name=f"v_grouped{j}", align_bytes=64)
            nc.scalar.copy(
                grouped[:].rearrange("p c t -> p (c t)").bitcast(F32).rearrange("p (c u) -> p c u", u=2),
                turned[:].rearrange("p u c -> p c u"),
            )
            return grouped

        v_grouped = [value_block(0)]

        pat_bank = ps.tile([P, PACK, Q], F32, name="pat_bank", tag="bank_pat")
        for t in range(PACK):
            nc.tensor.transpose(pat_bank[:, t, :], pa[:, t * P : (t + 1) * P], ident[:])
        pa_os = sb.tile([P, PACK, Q], F32, name="pa_os", tag="listed0", align_bytes=64)
        for t in range(PACK):
            nc.scalar.activation(pa_os[:, t, :], pat_bank[:, t, :], ACT.Copy, scale=os_col[:, t : t + 1])

        half_s = sb.tile([P, I // 2], F32, name="half_s")
        nc.gpsimd.tensor_tensor(half_s[:], pa[:, 0 : I // 2], pa[:, I // 2 : I], ALU.add)
        quarter_s = sb.tile([P, G, HALVES], F32, name="quarter_s")
        nc.gpsimd.tensor_tensor(quarter_s[:].rearrange("p g h -> p (g h)"), half_s[:, 0:P], half_s[:, P : 2 * P], ALU.add)
        page_s = sb.tile([P, G], F32, name="page_s")
        nc.gpsimd.tensor_tensor(page_s[:], quarter_s[:, :, 0], quarter_s[:, :, 1], ALU.add)
        tb_sum = page_sum(sum_banks[1], sb.tile([P, G], F32, name="tb_sum"))

        v_grouped.append(value_block(1))

        sig2 = after_gather(1, 1024, [P, G], F32, "sig2")
        nc.vector.scalar_tensor_tensor(sig2[:], th[:], 1.0, num, ALU.add, ALU.mult)
        inv_s = after_gather(1, 3072, [P, G], F32, "inv_s")
        nc.vector.reciprocal(inv_s[:], page_s[:])
        neg_tq = sb.tile([P, G], F32, name="neg_tq")
        neg_tz = sb.tile([P, 1], F32, name="neg_tz")
        nc.vector.scalar_tensor_tensor(neg_tq[:], tb_sum[:], -1.5 / PAGE, sig2[:], ALU.mult, ALU.mult, accum_out=neg_tz[:])
        inv_z = after_gather(1, 4096, [P, 1], F32, "inv_z")
        nc.vector.reciprocal(inv_z[:], z[:])
        v_mx = [quantize(v_grouped[0], "v0", behind=1)]

        q0 = sb.tile([P, G], F32, name="q0")
        nc.gpsimd.tensor_tensor(q0[:], log_part[:], pos[:], ALU.add)
        q0tz = sb.tile([P, G], F32, name="q0tz")
        nc.gpsimd.tensor_scalar(q0tz[:], q0[:], neg_tz[:], inv_z[:], ALU.mult, ALU.mult)
        inv_sz = sb.tile([P, G], F32, name="inv_sz")
        nc.gpsimd.tensor_scalar(inv_sz[:], inv_s[:], inv_z[:], 1.0, ALU.mult, ALU.mult)
        top = sb.tile([P, G], F32, name="top")
        nc.gpsimd.tensor_tensor(top[:], q0tz[:], neg_tq[:], ALU.subtract)
        tr2 = sb.tile([P, G, HALVES], F32, name="tr2", align_bytes=64)
        nc.gpsimd.tensor_tensor(
            tr2[:],
            top[:].unsqueeze(2).to_broadcast([P, G, HALVES]),
            inv_sz[:].unsqueeze(2).to_broadcast([P, G, HALVES]),
            ALU.mult,
        )
        v_grouped.append(value_block(2))
        tr_bank = ps.tile([P, Q], F32, name="tr_bank", tag="bank_b")
        nc.tensor.transpose(tr_bank[:], tr2[:].rearrange("p g h -> p (g h)"), ident[:])
        v_grouped.append(value_block(3))
        w_grouped = after_gather(3, 1024, [P, Q, PACK], BF16, "w_grouped")
        nc.vector.tensor_tensor(
            w_grouped[:], tr_bank[:].unsqueeze(2).to_broadcast([P, Q, PACK]), pa_os[:].rearrange("p t q -> p q t"), ALU.mult
        )
        v_mx.append(quantize(v_grouped[1], "v1", behind=3))
        w_mx = quantize(w_grouped, "w")
        v_mx.append(quantize(v_grouped[2], "v2", behind=3, at=2048))
        v_mx.append(quantize(v_grouped[3], "v3"))

        for first, count, tag, copy in (
            (0, 2, "bank_a", nc.scalar.copy),
            (2, 1, "bank_pat", nc.vector.tensor_copy),
            (3, 1, "bank_tb", nc.vector.tensor_copy),
        ):
            o_bank = ps.tile([P, count * P], F32, name=f"o_bank{first}", tag=tag)
            for j in range(count):
                product(o_bank[:, j * P : (j + 1) * P], w_mx, v_mx[first + j][0][:], v_mx[first + j][1][:])
            o_rows = sb.tile([P, count * P], F32, name=f"o_rows{first}")
            copy(o_rows[:], o_bank[:])
            nc.sync.dma_start(out[:, first * P : (first + count) * P], o_rows[:])
